import numpy as np
import ml_dtypes


def mxq(x, axis, fmt="e4m3"):
    dtype, down = {"e4m3": (ml_dtypes.float8_e4m3fn, 7), "e5m2": (ml_dtypes.float8_e5m2, 14)}[fmt]
    v = np.moveaxis(np.asarray(x, np.float32).astype(ml_dtypes.bfloat16).astype(np.float64), axis, -1)
    blocks = v.reshape(v.shape[:-1] + (-1, 32))
    amax = np.abs(blocks).max(-1, keepdims=True)
    byte = np.maximum(np.where(amax > 0, np.frexp(amax)[1] - 1 + 127, 0) - down, 1)
    scale = np.exp2(byte - 127.0)
    codes = (blocks / scale).astype(np.float32).astype(dtype).astype(np.float64)
    return np.moveaxis((codes * scale).reshape(v.shape), -1, axis)


WIDE = False


def mx_kscale(k):
    if not WIDE:
        return np.ones(k)
    levels = np.array([30, -30])
    if k % 512:
        return np.exp2(np.random.permutation(np.resize(levels, k // 32))).repeat(32)
    a = np.empty((k // 512, 16))
    for p in range(k // 512):
        a[p, :8] = np.random.permutation(np.resize(levels, 8))
        for g in range(8):
            far = levels[np.abs(levels - a[p, g]) >= 10]
            a[p, g + 8] = far[np.random.randint(len(far))]
    return np.exp2(a.ravel()).repeat(32)


def f64(x):
    return np.asarray(x).astype(np.float64)


def striped(idx):
    return np.tile(np.asarray(idx).reshape(-1, 16).T, (8, 1)).astype(np.uint16)


def unstriped(offs):
    return offs[:16].T.reshape(-1).astype(np.int64)


E2M1 = np.array([0.0, 0.5, 1.0, 1.5, 2.0, 3.0, 4.0, 6.0, -0.0, -0.5, -1.0, -1.5, -2.0, -3.0, -4.0, -6.0])


def pack_weight(w, fmt):
    k, n = w.shape
    w = f64(np.asarray(w, np.float32).astype(ml_dtypes.bfloat16)).reshape(k // 32, 32, n)
    amax = np.abs(w).max(1)
    if fmt in ("e4m3", "e5m2"):
        byte = np.frexp(amax)[1] - 1 + 127 - (7 if fmt == "e4m3" else 14)
    else:
        mant, ex = np.frexp(amax / 6.0)
        byte = np.where(mant > 0.5, ex, ex - 1) + 127
    byte = np.clip(np.where(amax > 0, byte, 1), 1, 254)
    scaled = (w * np.exp2(127.0 - byte)[:, None, :]).reshape(k, n).astype(np.float32)
    by_word = np.ascontiguousarray(scaled.reshape(k // 512, 128, 4, n).transpose(0, 1, 3, 2))
    if fmt in ("e4m3", "e5m2"):
        words = by_word.astype(ml_dtypes.float8_e4m3fn if fmt == "e4m3" else ml_dtypes.float8_e5m2).view(np.uint8)
    else:
        c = by_word.astype(ml_dtypes.float4_e2m1fn).view(np.uint8) & 0xF
        words = (c[..., 0::2] | (c[..., 1::2] << 4)).reshape(k // 512, 128, 2 * n)
    return np.ascontiguousarray(words), np.ascontiguousarray(byte.astype(np.uint8).reshape(k // 512, 16, n))


def unpack_weight(words, scales, fmt):
    g, _, n = scales.shape
    words = np.ascontiguousarray(words).reshape(g, 128, n, -1)
    if fmt in ("e4m3", "e5m2"):
        vals = words.view(ml_dtypes.float8_e4m3fn if fmt == "e4m3" else ml_dtypes.float8_e5m2).astype(np.float64)
    else:
        nib = np.empty((g, 128, n, 4), np.uint8)
        nib[..., 0::2] = words & 0xF
        nib[..., 1::2] = words >> 4
        vals = E2M1[nib]
    vals = vals * np.repeat(np.exp2(scales.astype(np.float64) - 127.0), 8, axis=1)[..., None]
    return vals.transpose(0, 1, 3, 2).reshape(g * 512, n)


def sigmoid(v):
    return 1.0 / (1.0 + np.exp(-v))


K, T, J, R, O, N, L, E = 512, 2048, 256, 512, 128, 256, 512, 1024


def setup_inputs():
    n = np.random.standard_normal
    idx = np.random.permutation(T)[:J]
    idx2 = np.random.permutation(T)[:J]
    idx3 = np.random.permutation(J)[:O]
    idx4 = np.random.permutation(J)[:O]
    idx5 = np.random.permutation(E)[:O]
    fk = mx_kscale(K)
    fr = mx_kscale(R)
    fl = mx_kscale(L)
    xtp = pack_weight(n((K, T)) / fk[:, None], "e4m3")
    wp = pack_weight(n((K, R)) * 1 / np.sqrt(K) * fk[:, None], "e2m1")
    w2p = pack_weight(n((K, R)) * 1 / np.sqrt(K) * fk[:, None] * fr, "e5m2")
    wbp = pack_weight(n((R, N)) * 1 / np.sqrt(R) / fr[:, None], "e5m2")
    sxp = pack_weight(n((L, O)) / fl[:, None], "e2m1")
    wsp = pack_weight(n((L, N)) * 1 / np.sqrt(L) * fl[:, None], "e5m2")
    return {
        "xt_words": xtp[0],
        "xt_scales": xtp[1],
        "w_words": wp[0],
        "w_scales": wp[1],
        "w2_words": w2p[0],
        "w2_scales": w2p[1],
        "sg": (np.random.uniform(0.6, 1.6, (R, 1))).astype(np.float32),
        "bg": (np.random.uniform(-1.0, 1.0, (R, 1))).astype(np.float32),
        "wb_words": wbp[0],
        "wb_scales": wbp[1],
        "sx_words": sxp[0],
        "sx_scales": sxp[1],
        "ws_words": wsp[0],
        "ws_scales": wsp[1],
        "offs": striped(idx),
        "offs2": striped(idx2),
        "offs3": striped(idx3),
        "offs4": striped(idx4),
        "offs5": striped(idx5),
    }


def reference(xt_words, xt_scales, w_words, w_scales, w2_words, w2_scales, sg, bg, wb_words, wb_scales, sx_words, sx_scales, ws_words, ws_scales, offs, offs2, offs3, offs4, offs5):
    idx = unstriped(offs)
    idx2 = unstriped(offs2)
    idx3 = unstriped(offs3)
    idx4 = unstriped(offs4)
    idx5 = unstriped(offs5)
    xtu = unpack_weight(xt_words, xt_scales, "e4m3")
    wu = unpack_weight(w_words, w_scales, "e2m1")
    w2u = unpack_weight(w2_words, w2_scales, "e5m2")
    wbu = unpack_weight(wb_words, wb_scales, "e5m2")
    sxu = unpack_weight(sx_words, sx_scales, "e2m1")
    wsu = unpack_weight(ws_words, ws_scales, "e5m2")
    xtidxg = xtu[:, idx]
    a = wu.T @ xtidxg
    xtidx2g = xtu[:, idx2]
    b = w2u.T @ xtidx2g
    hid = b[:, idx4] * sigmoid(a[:, idx3] * f64(sg) + f64(bg))
    hidq = mxq(hid, 0, "e4m3")
    p = wbu.T @ hidq + wsu.T @ sxu
    y = np.zeros((N, E))
    y[:, idx5] = p
    return y

@@ -1,0 +1,205 @@
+from contextlib import ExitStack
+
+import concourse.mybir as mybir
+
+K, T, J, R, O, N, L, E = 512, 2048, 256, 512, 128, 256, 512, 1024
+FLOPS = 2 * (2 * K * R * J + R * N * O + L * N * O)
+
+F32 = mybir.dt.float32
+BF16 = mybir.dt.bfloat16
+I32 = mybir.dt.int32
+U32 = mybir.dt.uint32
+U16 = mybir.dt.uint16
+U8 = mybir.dt.uint8
+E4M3 = mybir.dt.float8_e4m3fn_x4
+E5M2 = mybir.dt.float8_e5m2_x4
+E2M1 = mybir.dt.float4_e2m1fn_x4
+ACT = mybir.ActivationFunctionType
+MULT = mybir.AluOpType.mult
+
+P = 128
+PACK = 4
+QUADS = 4
+QUAD = 32
+LINE = 16
+
+
+def load_plane(queues, plane, scales):
+    for q, queue in enumerate(queues):
+        queue.dma_start(
+            out=plane[QUAD * q : QUAD * q + PACK, :].bitcast(I32),
+            in_=scales[0, PACK * q : PACK * q + PACK, :].bitcast(I32),
+        )
+
+
+def stage_rows(queue, plane, scales):
+    queue.dma_start(out=plane[0 : QUADS * PACK, :].bitcast(I32), in_=scales[0].bitcast(I32))
+
+
+def spread_rows(queue, plane):
+    for q in range(1, QUADS):
+        queue.dma_start(
+            out=plane[QUAD * q : QUAD * q + PACK, :].bitcast(I32),
+            in_=plane[PACK * q : PACK * q + PACK, :].bitcast(I32),
+        )
+
+
+def deal(engine, dealt, raw, run):
+    engine.tensor_copy(
+        out=dealt.rearrange("p (t c i) -> p c t i", t=PACK, i=run),
+        in_=raw.rearrange("p (c i t) -> p c t i", t=PACK, i=run),
+    )
+
+
+def words_of(dram):
+    return dram[0].rearrange("p n t -> p (n t)").bitcast(I32)
+
+
+def tile_list_ahead_gatefetch_skip_scattered_kernel(
+    tc, xt_words, xt_scales, w_words, w_scales, w2_words, w2_scales, sg, bg, wb_words, wb_scales,
+    sx_words, sx_scales, ws_words, ws_scales, offs, offs2, offs3, offs4, offs5, out,
+):
+    nc = tc.nc
+    with ExitStack() as ctx:
+        keep = ctx.enter_context(tc.tile_pool(name="keep", bufs=1))
+        psum = ctx.enter_context(tc.psum_pool(name="psum", bufs=1))
+
+        def tile(shape, dtype, name):
+            return keep.tile(shape, dtype, name=name, align_bytes=64)
+
+        list1 = tile([P, J // 16], U16, "list1")
+        list2 = tile([P, J // 16], U16, "list2")
+        list3 = tile([P, O // 16], U16, "list3")
+        list4 = tile([P, O // 16], U16, "list4")
+        list5 = tile([P, O // 16], U16, "list5")
+        x_words = tile([P, T], U32, "x_words")
+        x_plane = tile([P, T], U8, "x_plane")
+        w_raw = tile([P, R], U16, "w_raw")
+        w2_raw = tile([P, R], U32, "w2_raw")
+        w_plane_raw = tile([P, R], U8, "w_plane_raw")
+        w2_plane_raw = tile([P, R], U8, "w2_plane_raw")
+        late_planes = tile([P, N + N + O], U8, "late_planes")
+        wb_plane = late_planes[:, 0:N]
+        ws_plane = late_planes[:, N : 2 * N]
+        sx_plane = late_planes[:, 2 * N : 2 * N + O]
+        wb_codes = tile([P, N], U32, "wb_codes")
+        ws_codes = tile([P, N], U32, "ws_codes")
+        sx_codes = tile([P, O], U16, "sx_codes")
+        slope = tile([P, PACK], F32, "slope")
+        offset = tile([P, PACK], F32, "offset")
+        pages = [tile([P, E], F32, f"page{h}") for h in range(N // P)]
+
+        nc.gpsimd.memset(w2_plane_raw[:].bitcast(I32), 0)
+        nc.vector.memset(x_plane[:].bitcast(I32), 0)
+        for page in pages:
+            nc.vector.memset(page[:], 0.0)
+        nc.vector.memset(w_plane_raw[:].bitcast(I32), 0)
+        nc.vector.memset(late_planes[:].bitcast(I32), 0)
+
+        nc.sync.dma_start(list1[:], offs)
+        nc.scalar.dma_start(out=w_raw[:].bitcast(I32), in_=w_words[0].bitcast(I32))
+        nc.sync.dma_start(list2[:], offs2)
+        load_plane((nc.sync, nc.sync, nc.scalar, nc.scalar), x_plane, xt_scales)
+        nc.sync.dma_start(out=x_words[:].bitcast(I32), in_=words_of(xt_words))
+        load_plane((nc.scalar,) * QUADS, w_plane_raw, w_scales)
+        nc.sync.dma_start(out=w2_raw[:].bitcast(I32), in_=words_of(w2_words))
+        nc.sync.dma_start(list3[:], offs3)
+        nc.sync.dma_start(list4[:], offs4)
+        stage_rows(nc.gpsimd, w2_plane_raw[:], w2_scales)
+        nc.gpsimd.dma_start(out=slope[:], in_=sg.rearrange("(p t) o -> p (t o)", t=PACK))
+        nc.gpsimd.dma_start(out=offset[:], in_=bg.rearrange("(p t) o -> p (t o)", t=PACK))
+
+        x1_plane = tile([P, J], U8, "x1_plane")
+        x2_plane = tile([P, J], U8, "x2_plane")
+        x1_codes = tile([P, J], U32, "x1_codes")
+        x2_codes = tile([P, J], U32, "x2_codes")
+        w_codes = tile([P, R], U16, "w_codes")
+        w2_codes = tile([P, R], U32, "w2_codes")
+        w_plane = tile([P, R], U8, "w_plane")
+        w2_plane = tile([P, R], U8, "w2_plane")
+
+        deal(nc.vector, w_codes[:], w_raw[:], LINE // 2)
+        nc.vector.tensor_copy(out=x1_plane[:], in_=x_plane[:].indirect(list1[:]))
+        nc.vector.tensor_copy(out=x2_plane[:], in_=x_plane[:].indirect(list2[:]))
+        deal(nc.gpsimd, w2_plane[:], w2_plane_raw[:], LINE)
+        for t in range(PACK):
+            nc.gpsimd.tensor_copy(
+                out=w_plane[:, P * t : P * (t + 1)],
+                in_=w_plane_raw[:].rearrange("p (m t) -> p t m", t=PACK)[:, t, :],
+            )
+        spread_rows(nc.sync, w2_plane)
+        for plane, scales in ((ws_plane, ws_scales), (sx_plane, sx_scales), (wb_plane, wb_scales)):
+            stage_rows(nc.sync, plane, scales)
+        nc.sync.dma_start(out=ws_codes[:].bitcast(I32), in_=words_of(ws_words))
+        nc.sync.dma_start(out=sx_codes[:].bitcast(I32), in_=sx_words[0].bitcast(I32))
+        spread_rows(nc.sync, late_planes)
+        nc.sync.dma_start(out=wb_codes[:].bitcast(I32), in_=words_of(wb_words))
+        nc.sync.dma_start(list5[:], offs5)
+        nc.vector.tensor_copy(out=x1_codes[:], in_=x_words[:].indirect(list1[:]))
+        nc.vector.tensor_copy(out=x2_codes[:], in_=x_words[:].indirect(list2[:]))
+
+        a_banks = [psum.tile([P, J], F32, name=f"a_bank{t}", tag=f"bank{t}") for t in range(PACK)]
+        for t in range(PACK):
+            cols = slice(P * t, P * (t + 1))
+            nc.tensor.matmul_mx(
+                out=a_banks[t][:], lhsT=w_codes[:, cols].bitcast(E2M1), lhsT_scale=w_plane[:, cols],
+                rhs=x1_codes[:].bitcast(E4M3), rhs_scale=x1_plane[:], start=True, stop=True,
+            )
+        a_rows = [keep.tile([P, J], F32, name=f"a_rows{t}", tag=f"a_rows{t % 2}", align_bytes=64) for t in range(PACK)]
+        gates = [tile([P, O], F32, f"gate{t}") for t in range(PACK)]
+        nc.vector.tensor_copy(out=a_rows[0][:], in_=a_banks[0][:])
+        deal(nc.vector, w2_codes[:], w2_raw[:], LINE // 4)
+        nc.vector.tensor_copy(out=a_rows[1][:], in_=a_banks[1][:])
+        for t in range(PACK):
+            if t > 1:
+                nc.scalar.copy(out=a_rows[t][:], in_=a_banks[t][:])
+            nc.scalar.activation(
+                out=gates[t][:], in_=a_rows[t][:].indirect(list3[:]), func=ACT.Sigmoid,
+                bias=offset[:, t : t + 1], scale=slope[:, t : t + 1],
+            )
+
+        b_banks = [psum.tile([P, J], F32, name=f"b_bank{t}", tag=f"bank{PACK + t}") for t in range(PACK)]
+        for t in range(PACK):
+            cols = slice(P * t, P * (t + 1))
+            nc.tensor.matmul_mx(
+                out=b_banks[t][:], lhsT=w2_codes[:, cols].bitcast(E5M2), lhsT_scale=w2_plane[:, cols],
+                rhs=x2_codes[:].bitcast(E4M3), rhs_scale=x2_plane[:], start=True, stop=True,
+            )
+        b_rows = [tile([P, J], F32, f"b_rows{t}") for t in range(PACK)]
+        hid = tile([P, PACK, O], F32, "hid")
+        for t in range(PACK):
+            if t < 2:
+                nc.vector.tensor_copy(out=b_rows[t][:], in_=b_banks[t][:])
+            else:
+                nc.scalar.copy(out=b_rows[t][:], in_=b_banks[t][:])
+            nc.vector.tensor_tensor(out=hid[:, t, :], in0=b_rows[t][:].indirect(list4[:]), in1=gates[t][:], op=MULT)
+
+        hid_bf = tile([P, O * PACK], BF16, "hid_bf")
+        nc.vector.tensor_copy(
+            out=hid_bf[:].rearrange("p (c i t) -> p c t i", t=PACK, i=4),
+            in_=hid[:].rearrange("p t (c i) -> p c t i", i=4),
+        )
+        hid_codes = tile([P, O], U32, "hid_codes")
+        hid_plane = tile([P, O], U8, "hid_plane")
+        nc.vector.quantize_mx(out=hid_codes[:].bitcast(E4M3), scales=hid_plane[:], in_=hid_bf[:])
+
+        p_banks = [psum.tile([P, O], F32, name=f"p_bank{h}", tag=f"bank{h}") for h in range(N // P)]
+        for h in range(N // P):
+            cols = slice(P * h, P * (h + 1))
+            nc.tensor.matmul_mx(
+                out=p_banks[h][:], lhsT=ws_codes[:, cols].bitcast(E5M2), lhsT_scale=ws_plane[:, cols],
+                rhs=sx_codes[:].bitcast(E2M1), rhs_scale=sx_plane, start=True, stop=False,
+            )
+        for h in range(N // P):
+            cols = slice(P * h, P * (h + 1))
+            nc.tensor.matmul_mx(
+                out=p_banks[h][:], lhsT=wb_codes[:, cols].bitcast(E5M2), lhsT_scale=wb_plane[:, cols],
+                rhs=hid_codes[:].bitcast(E4M3), rhs_scale=hid_plane[:], start=False, stop=True,
+            )
+        p_rows = [tile([P, O], F32, f"p_rows{h}") for h in range(N // P)]
+        nc.vector.tensor_copy(out=p_rows[0][:], in_=p_banks[0][:])
+        nc.vector.tensor_copy(out=pages[0][:].indirect(list5[:]), in_=p_rows[0][:])
+        nc.sync.dma_start(out=out[0:P, :], in_=pages[0][:])
+        nc.scalar.copy(out=p_rows[1][:], in_=p_banks[1][:])
+        nc.scalar.activation(out=pages[1][:].indirect(list5[:]), in_=p_rows[1][:], func=ACT.Copy)
+        nc.scalar.dma_start(out=out[P : 2 * P, :], in_=pages[1][:])

@@ -24,14 +24,6 @@ QUAD = 32
 LINE = 16
 
 
-def load_plane(queues, plane, scales):
-    for q, queue in enumerate(queues):
-        queue.dma_start(
-            out=plane[QUAD * q : QUAD * q + PACK, :].bitcast(I32),
-            in_=scales[0, PACK * q : PACK * q + PACK, :].bitcast(I32),
-        )
-
-
 def stage_rows(queue, plane, scales):
     queue.dma_start(out=plane[0 : QUADS * PACK, :].bitcast(I32), in_=scales[0].bitcast(I32))
 
@@ -64,8 +56,8 @@ def tile_list_ahead_gatefetch_skip_scattered_kernel(
         keep = ctx.enter_context(tc.tile_pool(name="keep", bufs=1))
         psum = ctx.enter_context(tc.psum_pool(name="psum", bufs=1))
 
-        def tile(shape, dtype, name):
-            return keep.tile(shape, dtype, name=name, align_bytes=64)
+        def tile(shape, dtype, name, tag=None):
+            return keep.tile(shape, dtype, name=name, tag=tag or name, align_bytes=64)
 
         list1 = tile([P, J // 16], U16, "list1")
         list2 = tile([P, J // 16], U16, "list2")
@@ -73,68 +65,71 @@ def tile_list_ahead_gatefetch_skip_scattered_kernel(
         list4 = tile([P, O // 16], U16, "list4")
         list5 = tile([P, O // 16], U16, "list5")
         x_words = tile([P, T], U32, "x_words")
-        x_plane = tile([P, T], U8, "x_plane")
-        w_raw = tile([P, R], U16, "w_raw")
+        x_plane = tile([P, T], U8, "x_plane", "x_plane_then_wb")
+        w_raw = tile([P, R], U16, "w_raw", "w_then_ws")
         w2_raw = tile([P, R], U32, "w2_raw")
-        w_plane_raw = tile([P, R], U8, "w_plane_raw")
-        w2_plane_raw = tile([P, R], U8, "w2_plane_raw")
-        late_planes = tile([P, N + N + O], U8, "late_planes")
-        wb_plane = late_planes[:, 0:N]
-        ws_plane = late_planes[:, N : 2 * N]
-        sx_plane = late_planes[:, 2 * N : 2 * N + O]
-        wb_codes = tile([P, N], U32, "wb_codes")
-        ws_codes = tile([P, N], U32, "ws_codes")
-        sx_codes = tile([P, O], U16, "sx_codes")
+        w_plane_raw = tile([P, R], U8, "w_plane_raw", "w_plane_then_sx")
+        w2_plane_raw = tile([P, R], U8, "w2_plane_raw", "w2_plane_then_late")
         slope = tile([P, PACK], F32, "slope")
         offset = tile([P, PACK], F32, "offset")
         pages = [tile([P, E], F32, f"page{h}") for h in range(N // P)]
 
-        nc.gpsimd.memset(w2_plane_raw[:].bitcast(I32), 0)
+        nc.vector.memset(w_plane_raw[:].bitcast(I32), 0)
         nc.vector.memset(x_plane[:].bitcast(I32), 0)
+        nc.vector.memset(w2_plane_raw[:].bitcast(I32), 0)
         for page in pages:
             nc.vector.memset(page[:], 0.0)
-        nc.vector.memset(w_plane_raw[:].bitcast(I32), 0)
-        nc.vector.memset(late_planes[:].bitcast(I32), 0)
 
         nc.sync.dma_start(list1[:], offs)
-        nc.scalar.dma_start(out=w_raw[:].bitcast(I32), in_=w_words[0].bitcast(I32))
+        nc.scalar.dma_start(out=slope[:], in_=sg.rearrange("(p t) o -> p (t o)", t=PACK))
+        nc.gpsimd.dma_start(out=offset[:], in_=bg.rearrange("(p t) o -> p (t o)", t=PACK))
+        stage_rows(nc.sync, w_plane_raw[:], w_scales)
+        stage_rows(nc.scalar, x_plane[:], xt_scales)
         nc.sync.dma_start(list2[:], offs2)
-        load_plane((nc.sync, nc.sync, nc.scalar, nc.scalar), x_plane, xt_scales)
-        nc.sync.dma_start(out=x_words[:].bitcast(I32), in_=words_of(xt_words))
-        load_plane((nc.scalar,) * QUADS, w_plane_raw, w_scales)
-        nc.sync.dma_start(out=w2_raw[:].bitcast(I32), in_=words_of(w2_words))
+        nc.scalar.dma_start(out=w_raw[:].bitcast(I32), in_=w_words[0].bitcast(I32))
+        stage_rows(nc.sync, w2_plane_raw[:], w2_scales)
+        nc.scalar.dma_start(out=x_words[:].bitcast(I32), in_=words_of(xt_words))
+        nc.scalar.dma_start(out=w2_raw[:].bitcast(I32), in_=words_of(w2_words))
         nc.sync.dma_start(list3[:], offs3)
         nc.sync.dma_start(list4[:], offs4)
-        stage_rows(nc.gpsimd, w2_plane_raw[:], w2_scales)
-        nc.gpsimd.dma_start(out=slope[:], in_=sg.rearrange("(p t) o -> p (t o)", t=PACK))
-        nc.gpsimd.dma_start(out=offset[:], in_=bg.rearrange("(p t) o -> p (t o)", t=PACK))
+        nc.sync.dma_start(list5[:], offs5)
 
-        x1_plane = tile([P, J], U8, "x1_plane")
-        x2_plane = tile([P, J], U8, "x2_plane")
+        x1_rows = tile([P, J], U8, "x1_rows")
+        x2_rows = tile([P, J], U8, "x2_rows")
         x1_codes = tile([P, J], U32, "x1_codes")
         x2_codes = tile([P, J], U32, "x2_codes")
         w_codes = tile([P, R], U16, "w_codes")
         w2_codes = tile([P, R], U32, "w2_codes")
-        w_plane = tile([P, R], U8, "w_plane")
-        w2_plane = tile([P, R], U8, "w2_plane")
+        a_planes = tile([P, R + J], U8, "a_planes")
+        b_planes = tile([P, R + J], U8, "b_planes")
+        w_plane, x1_plane = a_planes[:, 0:R], a_planes[:, R : R + J]
+        w2_plane, x2_plane = b_planes[:, 0:R], b_planes[:, R : R + J]
 
+        deal(nc.vector, w_plane, w_plane_raw[:], LINE)
+        nc.vector.tensor_copy(out=x1_rows[:], in_=x_plane[:].indirect(list1[:]))
+        nc.vector.tensor_copy(out=x1_plane.bitcast(I32), in_=x1_rows[:].bitcast(I32))
+        spread_rows(nc.sync, a_planes)
         deal(nc.vector, w_codes[:], w_raw[:], LINE // 2)
-        nc.vector.tensor_copy(out=x1_plane[:], in_=x_plane[:].indirect(list1[:]))
-        nc.vector.tensor_copy(out=x2_plane[:], in_=x_plane[:].indirect(list2[:]))
-        deal(nc.gpsimd, w2_plane[:], w2_plane_raw[:], LINE)
-        for t in range(PACK):
-            nc.gpsimd.tensor_copy(
-                out=w_plane[:, P * t : P * (t + 1)],
-                in_=w_plane_raw[:].rearrange("p (m t) -> p t m", t=PACK)[:, t, :],
-            )
-        spread_rows(nc.sync, w2_plane)
+        nc.vector.tensor_copy(out=x2_rows[:], in_=x_plane[:].indirect(list2[:]))
+        deal(nc.vector, w2_plane, w2_plane_raw[:], LINE)
+        nc.vector.tensor_copy(out=x2_plane.bitcast(I32), in_=x2_rows[:].bitcast(I32))
+        spread_rows(nc.sync, b_planes)
+
+        late_planes = tile([P, N + N + O], U8, "late_planes", "w2_plane_then_late")
+        wb_plane = late_planes[:, 0:N]
+        ws_plane = late_planes[:, N : 2 * N]
+        sx_plane = late_planes[:, 2 * N : 2 * N + O]
+        wb_codes = tile([P, N], U32, "wb_codes", "x_plane_then_wb")
+        ws_codes = tile([P, N], U32, "ws_codes", "w_then_ws")
+        sx_codes = tile([P, O], U16, "sx_codes", "w_plane_then_sx")
+        nc.gpsimd.memset(late_planes[:].bitcast(I32), 0)
         for plane, scales in ((ws_plane, ws_scales), (sx_plane, sx_scales), (wb_plane, wb_scales)):
             stage_rows(nc.sync, plane, scales)
         nc.sync.dma_start(out=ws_codes[:].bitcast(I32), in_=words_of(ws_words))
         nc.sync.dma_start(out=sx_codes[:].bitcast(I32), in_=sx_words[0].bitcast(I32))
         spread_rows(nc.sync, late_planes)
         nc.sync.dma_start(out=wb_codes[:].bitcast(I32), in_=words_of(wb_words))
-        nc.sync.dma_start(list5[:], offs5)
+
         nc.vector.tensor_copy(out=x1_codes[:], in_=x_words[:].indirect(list1[:]))
         nc.vector.tensor_copy(out=x2_codes[:], in_=x_words[:].indirect(list2[:]))
 
@@ -143,7 +138,7 @@ def tile_list_ahead_gatefetch_skip_scattered_kernel(
             cols = slice(P * t, P * (t + 1))
             nc.tensor.matmul_mx(
                 out=a_banks[t][:], lhsT=w_codes[:, cols].bitcast(E2M1), lhsT_scale=w_plane[:, cols],
-                rhs=x1_codes[:].bitcast(E4M3), rhs_scale=x1_plane[:], start=True, stop=True,
+                rhs=x1_codes[:].bitcast(E4M3), rhs_scale=x1_plane, start=True, stop=True,
             )
         a_rows = [keep.tile([P, J], F32, name=f"a_rows{t}", tag=f"a_rows{t % 2}", align_bytes=64) for t in range(PACK)]
         gates = [tile([P, O], F32, f"gate{t}") for t in range(PACK)]
@@ -163,7 +158,7 @@ def tile_list_ahead_gatefetch_skip_scattered_kernel(
             cols = slice(P * t, P * (t + 1))
             nc.tensor.matmul_mx(
                 out=b_banks[t][:], lhsT=w2_codes[:, cols].bitcast(E5M2), lhsT_scale=w2_plane[:, cols],
-                rhs=x2_codes[:].bitcast(E4M3), rhs_scale=x2_plane[:], start=True, stop=True,
+                rhs=x2_codes[:].bitcast(E4M3), rhs_scale=x2_plane, start=True, stop=True,
             )
         b_rows = [tile([P, J], F32, f"b_rows{t}") for t in range(PACK)]
         hid = tile([P, PACK, O], F32, "hid")

@@ -64,21 +64,18 @@ def tile_list_ahead_gatefetch_skip_scattered_kernel(
         list3 = tile([P, O // 16], U16, "list3")
         list4 = tile([P, O // 16], U16, "list4")
         list5 = tile([P, O // 16], U16, "list5")
-        x_words = tile([P, T], U32, "x_words")
-        x_plane = tile([P, T], U8, "x_plane", "x_plane_then_wb")
-        w_raw = tile([P, R], U16, "w_raw", "w_then_ws")
-        w2_raw = tile([P, R], U32, "w2_raw")
-        w_plane_raw = tile([P, R], U8, "w_plane_raw", "w_plane_then_sx")
+        x_words = tile([P, T], U32, "x_words", "x_words_then_ws")
+        x_plane = tile([P, T], U8, "x_plane")
+        w_raw = tile([P, R], U16, "w_raw")
+        w2_raw = tile([P, R], U32, "w2_raw", "w2_then_wb")
+        w_plane_raw = tile([P, R], U8, "w_plane_raw")
         w2_plane_raw = tile([P, R], U8, "w2_plane_raw", "w2_plane_then_late")
         slope = tile([P, PACK], F32, "slope")
         offset = tile([P, PACK], F32, "offset")
-        pages = [tile([P, E], F32, f"page{h}") for h in range(N // P)]
 
-        nc.vector.memset(w_plane_raw[:].bitcast(I32), 0)
+        nc.gpsimd.memset(w_plane_raw[:].bitcast(I32), 0)
         nc.vector.memset(x_plane[:].bitcast(I32), 0)
         nc.vector.memset(w2_plane_raw[:].bitcast(I32), 0)
-        for page in pages:
-            nc.vector.memset(page[:], 0.0)
 
         nc.sync.dma_start(list1[:], offs)
         nc.scalar.dma_start(out=slope[:], in_=sg.rearrange("(p t) o -> p (t o)", t=PACK))
@@ -94,22 +91,22 @@ def tile_list_ahead_gatefetch_skip_scattered_kernel(
         nc.sync.dma_start(list4[:], offs4)
         nc.sync.dma_start(list5[:], offs5)
 
-        x1_rows = tile([P, J], U8, "x1_rows")
-        x2_rows = tile([P, J], U8, "x2_rows")
-        x1_codes = tile([P, J], U32, "x1_codes")
+        x1_rows = tile([P, J], U8, "x1_rows", "x_rows_then_sx")
+        x1_codes = tile([P, J], U32, "x1_codes", "x1_then_page1")
         x2_codes = tile([P, J], U32, "x2_codes")
-        w_codes = tile([P, R], U16, "w_codes")
+        w_codes = tile([P, R], U16, "w_codes", "w_then_page0")
         w2_codes = tile([P, R], U32, "w2_codes")
         a_planes = tile([P, R + J], U8, "a_planes")
         b_planes = tile([P, R + J], U8, "b_planes")
         w_plane, x1_plane = a_planes[:, 0:R], a_planes[:, R : R + J]
         w2_plane, x2_plane = b_planes[:, 0:R], b_planes[:, R : R + J]
 
-        deal(nc.vector, w_plane, w_plane_raw[:], LINE)
         nc.vector.tensor_copy(out=x1_rows[:], in_=x_plane[:].indirect(list1[:]))
+        deal(nc.vector, w_plane, w_plane_raw[:], LINE)
         nc.vector.tensor_copy(out=x1_plane.bitcast(I32), in_=x1_rows[:].bitcast(I32))
         spread_rows(nc.sync, a_planes)
         deal(nc.vector, w_codes[:], w_raw[:], LINE // 2)
+        x2_rows = tile([P, J], U8, "x2_rows", "x_rows_then_sx")
         nc.vector.tensor_copy(out=x2_rows[:], in_=x_plane[:].indirect(list2[:]))
         deal(nc.vector, w2_plane, w2_plane_raw[:], LINE)
         nc.vector.tensor_copy(out=x2_plane.bitcast(I32), in_=x2_rows[:].bitcast(I32))
@@ -119,9 +116,9 @@ def tile_list_ahead_gatefetch_skip_scattered_kernel(
         wb_plane = late_planes[:, 0:N]
         ws_plane = late_planes[:, N : 2 * N]
         sx_plane = late_planes[:, 2 * N : 2 * N + O]
-        wb_codes = tile([P, N], U32, "wb_codes", "x_plane_then_wb")
-        ws_codes = tile([P, N], U32, "ws_codes", "w_then_ws")
-        sx_codes = tile([P, O], U16, "sx_codes", "w_plane_then_sx")
+        wb_codes = tile([P, N], U32, "wb_codes", "w2_then_wb")
+        ws_codes = tile([P, N], U32, "ws_codes", "x_words_then_ws")
+        sx_codes = tile([P, O], U16, "sx_codes", "x_rows_then_sx")
         nc.gpsimd.memset(late_planes[:].bitcast(I32), 0)
         for plane, scales in ((ws_plane, ws_scales), (sx_plane, sx_scales), (wb_plane, wb_scales)):
             stage_rows(nc.sync, plane, scales)
@@ -140,18 +137,15 @@ def tile_list_ahead_gatefetch_skip_scattered_kernel(
                 out=a_banks[t][:], lhsT=w_codes[:, cols].bitcast(E2M1), lhsT_scale=w_plane[:, cols],
                 rhs=x1_codes[:].bitcast(E4M3), rhs_scale=x1_plane, start=True, stop=True,
             )
-        a_rows = [keep.tile([P, J], F32, name=f"a_rows{t}", tag=f"a_rows{t % 2}", align_bytes=64) for t in range(PACK)]
+        a_rows = [keep.tile([P, J], F32, name=f"a_rows{t}", tag=f"a_rows{t % 3}", align_bytes=64) for t in range(PACK)]
         gates = [tile([P, O], F32, f"gate{t}") for t in range(PACK)]
-        nc.vector.tensor_copy(out=a_rows[0][:], in_=a_banks[0][:])
         deal(nc.vector, w2_codes[:], w2_raw[:], LINE // 4)
-        nc.vector.tensor_copy(out=a_rows[1][:], in_=a_banks[1][:])
-        for t in range(PACK):
-            if t > 1:
-                nc.scalar.copy(out=a_rows[t][:], in_=a_banks[t][:])
-            nc.scalar.activation(
-                out=gates[t][:], in_=a_rows[t][:].indirect(list3[:]), func=ACT.Sigmoid,
-                bias=offset[:, t : t + 1], scale=slope[:, t : t + 1],
-            )
+        for t in range(PACK - 1):
+            nc.vector.tensor_copy(out=a_rows[t][:], in_=a_banks[t][:])
+
+        pages = [tile([P, E], F32, "page0", "w_then_page0"), tile([P, E], F32, "page1", "x1_then_page1")]
+        for page in pages:
+            nc.gpsimd.memset(page[:], 0.0)
 
         b_banks = [psum.tile([P, J], F32, name=f"b_bank{t}", tag=f"bank{PACK + t}") for t in range(PACK)]
         for t in range(PACK):
@@ -162,11 +156,18 @@ def tile_list_ahead_gatefetch_skip_scattered_kernel(
             )
         b_rows = [tile([P, J], F32, f"b_rows{t}") for t in range(PACK)]
         hid = tile([P, PACK, O], F32, "hid")
+        last = PACK - 1
         for t in range(PACK):
-            if t < 2:
-                nc.vector.tensor_copy(out=b_rows[t][:], in_=b_banks[t][:])
-            else:
-                nc.scalar.copy(out=b_rows[t][:], in_=b_banks[t][:])
+            if t == last:
+                nc.scalar.copy(out=a_rows[last][:], in_=a_banks[last][:])
+            nc.scalar.activation(
+                out=gates[t][:], in_=a_rows[t][:].indirect(list3[:]), func=ACT.Sigmoid,
+                bias=offset[:, t : t + 1], scale=slope[:, t : t + 1],
+            )
+        for t in range(last):
+            nc.vector.tensor_copy(out=b_rows[t][:], in_=b_banks[t][:])
+        nc.scalar.copy(out=b_rows[last][:], in_=b_banks[last][:])
+        for t in range(PACK):
             nc.vector.tensor_tensor(out=hid[:, t, :], in0=b_rows[t][:].indirect(list4[:]), in1=gates[t][:], op=MULT)
 
         hid_bf = tile([P, O * PACK], BF16, "hid_bf")

@@ -28,8 +28,8 @@ def stage_rows(queue, plane, scales):
     queue.dma_start(out=plane[0 : QUADS * PACK, :].bitcast(I32), in_=scales[0].bitcast(I32))
 
 
-def spread_rows(queue, plane):
-    for q in range(1, QUADS):
+def spread_rows(queues, plane):
+    for q, queue in enumerate(queues, start=1):
         queue.dma_start(
             out=plane[QUAD * q : QUAD * q + PACK, :].bitcast(I32),
             in_=plane[PACK * q : PACK * q + PACK, :].bitcast(I32),
@@ -76,6 +76,9 @@ def tile_list_ahead_gatefetch_skip_scattered_kernel(
         nc.gpsimd.memset(w_plane_raw[:].bitcast(I32), 0)
         nc.vector.memset(x_plane[:].bitcast(I32), 0)
         nc.vector.memset(w2_plane_raw[:].bitcast(I32), 0)
+        pages = [tile([P, E], F32, f"page{h}") for h in range(N // P)]
+        for page in pages:
+            nc.vector.memset(page[:].bitcast(I32), 0)
 
         nc.sync.dma_start(list1[:], offs)
         nc.scalar.dma_start(out=slope[:], in_=sg.rearrange("(p t) o -> p (t o)", t=PACK))
@@ -92,25 +95,25 @@ def tile_list_ahead_gatefetch_skip_scattered_kernel(
         nc.sync.dma_start(list5[:], offs5)
 
         x1_rows = tile([P, J], U8, "x1_rows", "x_rows_then_sx")
-        x1_codes = tile([P, J], U32, "x1_codes", "x1_then_page1")
+        x1_codes = tile([P, J], U32, "x1_codes")
         x2_codes = tile([P, J], U32, "x2_codes")
-        w_codes = tile([P, R], U16, "w_codes", "w_then_page0")
+        w_codes = tile([P, R], U16, "w_codes")
         w2_codes = tile([P, R], U32, "w2_codes")
         a_planes = tile([P, R + J], U8, "a_planes")
         b_planes = tile([P, R + J], U8, "b_planes")
         w_plane, x1_plane = a_planes[:, 0:R], a_planes[:, R : R + J]
         w2_plane, x2_plane = b_planes[:, 0:R], b_planes[:, R : R + J]
 
-        nc.vector.tensor_copy(out=x1_rows[:], in_=x_plane[:].indirect(list1[:]))
         deal(nc.vector, w_plane, w_plane_raw[:], LINE)
+        nc.vector.tensor_copy(out=x1_rows[:], in_=x_plane[:].indirect(list1[:]))
         nc.vector.tensor_copy(out=x1_plane.bitcast(I32), in_=x1_rows[:].bitcast(I32))
-        spread_rows(nc.sync, a_planes)
+        spread_rows((nc.sync, nc.scalar, nc.sync), a_planes)
         deal(nc.vector, w_codes[:], w_raw[:], LINE // 2)
         x2_rows = tile([P, J], U8, "x2_rows", "x_rows_then_sx")
         nc.vector.tensor_copy(out=x2_rows[:], in_=x_plane[:].indirect(list2[:]))
         deal(nc.vector, w2_plane, w2_plane_raw[:], LINE)
         nc.vector.tensor_copy(out=x2_plane.bitcast(I32), in_=x2_rows[:].bitcast(I32))
-        spread_rows(nc.sync, b_planes)
+        spread_rows((nc.sync,) * 3, b_planes)
 
         late_planes = tile([P, N + N + O], U8, "late_planes", "w2_plane_then_late")
         wb_plane = late_planes[:, 0:N]
@@ -124,7 +127,7 @@ def tile_list_ahead_gatefetch_skip_scattered_kernel(
             stage_rows(nc.sync, plane, scales)
         nc.sync.dma_start(out=ws_codes[:].bitcast(I32), in_=words_of(ws_words))
         nc.sync.dma_start(out=sx_codes[:].bitcast(I32), in_=sx_words[0].bitcast(I32))
-        spread_rows(nc.sync, late_planes)
+        spread_rows((nc.sync,) * 3, late_planes)
         nc.sync.dma_start(out=wb_codes[:].bitcast(I32), in_=words_of(wb_words))
 
         nc.vector.tensor_copy(out=x1_codes[:], in_=x_words[:].indirect(list1[:]))
@@ -143,10 +146,6 @@ def tile_list_ahead_gatefetch_skip_scattered_kernel(
         for t in range(PACK - 1):
             nc.vector.tensor_copy(out=a_rows[t][:], in_=a_banks[t][:])
 
-        pages = [tile([P, E], F32, "page0", "w_then_page0"), tile([P, E], F32, "page1", "x1_then_page1")]
-        for page in pages:
-            nc.gpsimd.memset(page[:], 0.0)
-
         b_banks = [psum.tile([P, J], F32, name=f"b_bank{t}", tag=f"bank{PACK + t}") for t in range(PACK)]
         for t in range(PACK):
             cols = slice(P * t, P * (t + 1))
@@ -158,13 +157,15 @@ def tile_list_ahead_gatefetch_skip_scattered_kernel(
         hid = tile([P, PACK, O], F32, "hid")
         last = PACK - 1
         for t in range(PACK):
-            if t == last:
+            if t == 2:
                 nc.scalar.copy(out=a_rows[last][:], in_=a_banks[last][:])
+            if t == last:
+                nc.scalar.copy(out=b_rows[2][:], in_=b_banks[2][:])
             nc.scalar.activation(
                 out=gates[t][:], in_=a_rows[t][:].indirect(list3[:]), func=ACT.Sigmoid,
                 bias=offset[:, t : t + 1], scale=slope[:, t : t + 1],
             )
-        for t in range(last):
+        for t in range(2):
             nc.vector.tensor_copy(out=b_rows[t][:], in_=b_banks[t][:])
         nc.scalar.copy(out=b_rows[last][:], in_=b_banks[last][:])
         for t in range(PACK):

from contextlib import ExitStack

import concourse.mybir as mybir

K, T, J, R, O, N, L, E = 512, 2048, 256, 512, 128, 256, 512, 1024
FLOPS = 2 * (2 * K * R * J + R * N * O + L * N * O)

F32 = mybir.dt.float32
BF16 = mybir.dt.bfloat16
I32 = mybir.dt.int32
U32 = mybir.dt.uint32
U16 = mybir.dt.uint16
U8 = mybir.dt.uint8
E4M3 = mybir.dt.float8_e4m3fn_x4
E5M2 = mybir.dt.float8_e5m2_x4
E2M1 = mybir.dt.float4_e2m1fn_x4
ACT = mybir.ActivationFunctionType
MULT = mybir.AluOpType.mult

P = 128
PACK = 4
QUADS = 4
QUAD = 32
LINE = 16


def stage_rows(queue, plane, scales):
    queue.dma_start(out=plane[0 : QUADS * PACK, :].bitcast(I32), in_=scales[0].bitcast(I32))


def spread_rows(queues, plane):
    for q, queue in enumerate(queues, start=1):
        queue.dma_start(
            out=plane[QUAD * q : QUAD * q + PACK, :].bitcast(I32),
            in_=plane[PACK * q : PACK * q + PACK, :].bitcast(I32),
        )


def deal(engine, dealt, raw, run):
    engine.tensor_copy(
        out=dealt.rearrange("p (t c i) -> p c t i", t=PACK, i=run),
        in_=raw.rearrange("p (c i t) -> p c t i", t=PACK, i=run),
    )


def words_of(dram):
    return dram[0].rearrange("p n t -> p (n t)").bitcast(I32)


def tile_list_ahead_gatefetch_skip_scattered_kernel(
    tc, xt_words, xt_scales, w_words, w_scales, w2_words, w2_scales, sg, bg, wb_words, wb_scales,
    sx_words, sx_scales, ws_words, ws_scales, offs, offs2, offs3, offs4, offs5, out,
):
    nc = tc.nc
    with ExitStack() as ctx:
        keep = ctx.enter_context(tc.tile_pool(name="keep", bufs=1))
        psum = ctx.enter_context(tc.psum_pool(name="psum", bufs=1))

        def tile(shape, dtype, name, tag=None):
            return keep.tile(shape, dtype, name=name, tag=tag or name, align_bytes=64)

        list1 = tile([P, J // 16], U16, "list1")
        list2 = tile([P, J // 16], U16, "list2")
        list3 = tile([P, O // 16], U16, "list3")
        list4 = tile([P, O // 16], U16, "list4")
        list5 = tile([P, O // 16], U16, "list5")
        x_words = tile([P, T], U32, "x_words", "x_words_then_ws")
        x_plane = tile([P, T], U8, "x_plane")
        w_raw = tile([P, R], U16, "w_raw")
        w2_raw = tile([P, R], U32, "w2_raw", "w2_then_wb")
        w_plane_raw = tile([P, R], U8, "w_plane_raw")
        w2_plane_raw = tile([P, R], U8, "w2_plane_raw", "w2_plane_then_late")
        slope = tile([P, PACK], F32, "slope")
        offset = tile([P, PACK], F32, "offset")

        nc.gpsimd.memset(w_plane_raw[:].bitcast(I32), 0)
        nc.vector.memset(x_plane[:].bitcast(I32), 0)
        nc.vector.memset(w2_plane_raw[:].bitcast(I32), 0)
        pages = [tile([P, E], F32, f"page{h}") for h in range(N // P)]
        for page in pages:
            nc.vector.memset(page[:].bitcast(I32), 0)

        nc.sync.dma_start(list1[:], offs)
        nc.scalar.dma_start(out=slope[:], in_=sg.rearrange("(p t) o -> p (t o)", t=PACK))
        nc.gpsimd.dma_start(out=offset[:], in_=bg.rearrange("(p t) o -> p (t o)", t=PACK))
        stage_rows(nc.sync, w_plane_raw[:], w_scales)
        stage_rows(nc.scalar, x_plane[:], xt_scales)
        nc.sync.dma_start(list2[:], offs2)
        nc.scalar.dma_start(out=w_raw[:].bitcast(I32), in_=w_words[0].bitcast(I32))
        stage_rows(nc.sync, w2_plane_raw[:], w2_scales)
        nc.scalar.dma_start(out=x_words[:].bitcast(I32), in_=words_of(xt_words))
        nc.scalar.dma_start(out=w2_raw[:].bitcast(I32), in_=words_of(w2_words))
        nc.sync.dma_start(list3[:], offs3)
        nc.sync.dma_start(list4[:], offs4)
        nc.sync.dma_start(list5[:], offs5)

        x1_rows = tile([P, J], U8, "x1_rows", "x_rows_then_sx")
        x1_codes = tile([P, J], U32, "x1_codes")
        x2_codes = tile([P, J], U32, "x2_codes")
        w_codes = tile([P, R], U16, "w_codes")
        w2_codes = tile([P, R], U32, "w2_codes")
        a_planes = tile([P, R + J], U8, "a_planes")
        b_planes = tile([P, R + J], U8, "b_planes")
        w_plane, x1_plane = a_planes[:, 0:R], a_planes[:, R : R + J]
        w2_plane, x2_plane = b_planes[:, 0:R], b_planes[:, R : R + J]

        deal(nc.vector, w_plane, w_plane_raw[:], LINE)
        nc.vector.tensor_copy(out=x1_rows[:], in_=x_plane[:].indirect(list1[:]))
        nc.vector.tensor_copy(out=x1_plane.bitcast(I32), in_=x1_rows[:].bitcast(I32))
        spread_rows((nc.sync, nc.scalar, nc.sync), a_planes)
        deal(nc.vector, w_codes[:], w_raw[:], LINE // 2)
        x2_rows = tile([P, J], U8, "x2_rows", "x_rows_then_sx")
        nc.vector.tensor_copy(out=x2_rows[:], in_=x_plane[:].indirect(list2[:]))
        deal(nc.vector, w2_plane, w2_plane_raw[:], LINE)
        nc.vector.tensor_copy(out=x2_plane.bitcast(I32), in_=x2_rows[:].bitcast(I32))
        spread_rows((nc.sync,) * 3, b_planes)

        late_planes = tile([P, N + N + O], U8, "late_planes", "w2_plane_then_late")
        wb_plane = late_planes[:, 0:N]
        ws_plane = late_planes[:, N : 2 * N]
        sx_plane = late_planes[:, 2 * N : 2 * N + O]
        wb_codes = tile([P, N], U32, "wb_codes", "w2_then_wb")
        ws_codes = tile([P, N], U32, "ws_codes", "x_words_then_ws")
        sx_codes = tile([P, O], U16, "sx_codes", "x_rows_then_sx")
        nc.gpsimd.memset(late_planes[:].bitcast(I32), 0)
        for plane, scales in ((ws_plane, ws_scales), (sx_plane, sx_scales), (wb_plane, wb_scales)):
            stage_rows(nc.sync, plane, scales)
        nc.sync.dma_start(out=ws_codes[:].bitcast(I32), in_=words_of(ws_words))
        nc.sync.dma_start(out=sx_codes[:].bitcast(I32), in_=sx_words[0].bitcast(I32))
        spread_rows((nc.sync,) * 3, late_planes)
        nc.sync.dma_start(out=wb_codes[:].bitcast(I32), in_=words_of(wb_words))

        nc.vector.tensor_copy(out=x1_codes[:], in_=x_words[:].indirect(list1[:]))
        nc.vector.tensor_copy(out=x2_codes[:], in_=x_words[:].indirect(list2[:]))

        a_banks = [psum.tile([P, J], F32, name=f"a_bank{t}", tag=f"bank{t}") for t in range(PACK)]
        for t in range(PACK):
            cols = slice(P * t, P * (t + 1))
            nc.tensor.matmul_mx(
                out=a_banks[t][:], lhsT=w_codes[:, cols].bitcast(E2M1), lhsT_scale=w_plane[:, cols],
                rhs=x1_codes[:].bitcast(E4M3), rhs_scale=x1_plane, start=True, stop=True,
            )
        a_rows = [keep.tile([P, J], F32, name=f"a_rows{t}", tag=f"a_rows{t % 3}", align_bytes=64) for t in range(PACK)]
        gates = [tile([P, O], F32, f"gate{t}") for t in range(PACK)]
        deal(nc.vector, w2_codes[:], w2_raw[:], LINE // 4)
        for t in range(PACK - 1):
            nc.vector.tensor_copy(out=a_rows[t][:], in_=a_banks[t][:])

        b_banks = [psum.tile([P, J], F32, name=f"b_bank{t}", tag=f"bank{PACK + t}") for t in range(PACK)]
        for t in range(PACK):
            cols = slice(P * t, P * (t + 1))
            nc.tensor.matmul_mx(
                out=b_banks[t][:], lhsT=w2_codes[:, cols].bitcast(E5M2), lhsT_scale=w2_plane[:, cols],
                rhs=x2_codes[:].bitcast(E4M3), rhs_scale=x2_plane, start=True, stop=True,
            )
        b_rows = [tile([P, J], F32, f"b_rows{t}") for t in range(PACK)]
        hid = tile([P, PACK, O], F32, "hid")
        last = PACK - 1
        for t in range(PACK):
            if t == 2:
                nc.scalar.copy(out=a_rows[last][:], in_=a_banks[last][:])
            if t == last:
                nc.scalar.copy(out=b_rows[2][:], in_=b_banks[2][:])
            nc.scalar.activation(
                out=gates[t][:], in_=a_rows[t][:].indirect(list3[:]), func=ACT.Sigmoid,
                bias=offset[:, t : t + 1], scale=slope[:, t : t + 1],
            )
        for t in range(2):
            nc.vector.tensor_copy(out=b_rows[t][:], in_=b_banks[t][:])
        nc.scalar.copy(out=b_rows[last][:], in_=b_banks[last][:])
        for t in range(PACK):
            nc.vector.tensor_tensor(out=hid[:, t, :], in0=b_rows[t][:].indirect(list4[:]), in1=gates[t][:], op=MULT)

        hid_bf = tile([P, O * PACK], BF16, "hid_bf")
        nc.vector.tensor_copy(
            out=hid_bf[:].rearrange("p (c i t) -> p c t i", t=PACK, i=4),
            in_=hid[:].rearrange("p t (c i) -> p c t i", i=4),
        )
        hid_codes = tile([P, O], U32, "hid_codes")
        hid_plane = tile([P, O], U8, "hid_plane")
        nc.vector.quantize_mx(out=hid_codes[:].bitcast(E4M3), scales=hid_plane[:], in_=hid_bf[:])

        p_banks = [psum.tile([P, O], F32, name=f"p_bank{h}", tag=f"bank{h}") for h in range(N // P)]
        for h in range(N // P):
            cols = slice(P * h, P * (h + 1))
            nc.tensor.matmul_mx(
                out=p_banks[h][:], lhsT=ws_codes[:, cols].bitcast(E5M2), lhsT_scale=ws_plane[:, cols],
                rhs=sx_codes[:].bitcast(E2M1), rhs_scale=sx_plane, start=True, stop=False,
            )
        for h in range(N // P):
            cols = slice(P * h, P * (h + 1))
            nc.tensor.matmul_mx(
                out=p_banks[h][:], lhsT=wb_codes[:, cols].bitcast(E5M2), lhsT_scale=wb_plane[:, cols],
                rhs=hid_codes[:].bitcast(E4M3), rhs_scale=hid_plane[:], start=False, stop=True,
            )
        p_rows = [tile([P, O], F32, f"p_rows{h}") for h in range(N // P)]
        nc.vector.tensor_copy(out=p_rows[0][:], in_=p_banks[0][:])
        nc.vector.tensor_copy(out=pages[0][:].indirect(list5[:]), in_=p_rows[0][:])
        nc.sync.dma_start(out=out[0:P, :], in_=pages[0][:])
        nc.scalar.copy(out=p_rows[1][:], in_=p_banks[1][:])
        nc.scalar.activation(out=pages[1][:].indirect(list5[:]), in_=p_rows[1][:], func=ACT.Copy)
        nc.scalar.dma_start(out=out[P : 2 * P, :], in_=pages[1][:])
